import numpy as np
import ml_dtypes


def mxq(x, axis, fmt="e4m3"):
    dtype, down = {"e4m3": (ml_dtypes.float8_e4m3fn, 7), "e5m2": (ml_dtypes.float8_e5m2, 14)}[fmt]
    v = np.moveaxis(np.asarray(x, np.float32).astype(ml_dtypes.bfloat16).astype(np.float64), axis, -1)
    blocks = v.reshape(v.shape[:-1] + (-1, 32))
    amax = np.abs(blocks).max(-1, keepdims=True)
    byte = np.maximum(np.where(amax > 0, np.frexp(amax)[1] - 1 + 127, 0) - down, 1)
    scale = np.exp2(byte - 127.0)
    codes = (blocks / scale).astype(np.float32).astype(dtype).astype(np.float64)
    return np.moveaxis((codes * scale).reshape(v.shape), -1, axis)


WIDE = False


def mx_kscale(k):
    if not WIDE:
        return np.ones(k)
    levels = np.array([10, -10, 5, -5, 0])
    if k % 512:
        return np.exp2(np.random.permutation(np.resize(levels, k // 32))).repeat(32)
    a = np.empty((k // 512, 16))
    for p in range(k // 512):
        a[p, :8] = np.random.permutation(np.resize(levels, 8))
        for g in range(8):
            far = levels[np.abs(levels - a[p, g]) >= 10]
            a[p, g + 8] = far[np.random.randint(len(far))]
    return np.exp2(a.ravel()).repeat(32)


def f64(x):
    return np.asarray(x).astype(np.float64)


def striped(idx):
    return np.tile(idx.reshape(-1, 16).T, (8, 1)).astype(np.uint16)


def unstriped(offs):
    return offs[:16].T.reshape(-1).astype(np.int64)


E2M1 = np.array([0.0, 0.5, 1.0, 1.5, 2.0, 3.0, 4.0, 6.0, -0.0, -0.5, -1.0, -1.5, -2.0, -3.0, -4.0, -6.0])


def pack_fp4(w):
    k, n = w.shape
    w = f64(np.asarray(w, np.float32).astype(ml_dtypes.bfloat16)).reshape(k // 32, 32, n)
    amax = np.abs(w).max(1)
    mant, ex = np.frexp(amax / 6.0)
    byte = np.clip(np.where(amax > 0, np.where(mant > 0.5, ex, ex - 1) + 127, 1), 1, 254)
    scaled = (w * np.exp2(127.0 - byte)[:, None, :]).reshape(k, n).astype(np.float32)
    c = np.ascontiguousarray(scaled.reshape(k // 512, 128, 4, n).transpose(0, 1, 3, 2)).astype(ml_dtypes.float4_e2m1fn).view(np.uint8) & 0xF
    words = (c[..., 0::2] | (c[..., 1::2] << 4)).reshape(k // 512, 128, 2 * n)
    return np.ascontiguousarray(words), np.ascontiguousarray(byte.astype(np.uint8).reshape(k // 512, 16, n))


def unpack_fp4(words, scales):
    g, _, n = scales.shape
    words = np.ascontiguousarray(words).reshape(g, 128, n, 2)
    nib = np.empty((g, 128, n, 4), np.uint8)
    nib[..., 0::2] = words & 0xF
    nib[..., 1::2] = words >> 4
    vals = E2M1[nib] * np.repeat(np.exp2(scales.astype(np.float64) - 127.0), 8, axis=1)[..., None]
    return vals.transpose(0, 1, 3, 2).reshape(g * 512, n)


K, T, S, V, N = 512, 1024, 512, 256, 128
P = 2 ** 7


def setup_inputs():
    n = np.random.standard_normal
    s = mx_kscale(K)[:, None]
    packed_xT = pack_fp4(n((K, T)) * s)
    return {
        "x_words": packed_xT[0],
        "x_scales": packed_xT[1],
        "w1": (n((K, N)) / np.sqrt(K) / s).astype(np.float32),
        "fx": np.tile(np.random.uniform(0.05, 0.95, V), (P, 1)).astype(np.float32),
        "fy": np.tile(np.random.uniform(0.05, 0.95, V), (P, 1)).astype(np.float32),
        "offs": striped(np.random.permutation(T)[:S]),
        "c00": striped(np.random.permutation(S)[:V]),
        "c01": striped(np.random.permutation(S)[:V]),
        "c10": striped(np.random.permutation(S)[:V]),
        "c11": striped(np.random.permutation(S)[:V]),
    }


def reference(x_words, x_scales, w1, fx, fy, offs, c00, c01, c10, c11):
    xq = unpack_fp4(x_words, x_scales)[:, unstriped(offs)]
    y = mxq(f64(w1), 0, "e4m3").T @ xq
    top = y[:, unstriped(c00)] + (y[:, unstriped(c01)] - y[:, unstriped(c00)]) * f64(fx)[:1]
    low = y[:, unstriped(c10)] + (y[:, unstriped(c11)] - y[:, unstriped(c10)]) * f64(fx)[:1]
    return top + (low - top) * f64(fy)[:1]

@@ -1,0 +1,89 @@
+from contextlib import ExitStack
+
+import concourse.mybir as mybir
+
+K, T, S, V, N = 512, 1024, 512, 256, 128
+P = 128
+FLOPS = 2 * K * N * S
+
+F32 = mybir.dt.float32
+BF16 = mybir.dt.bfloat16
+I32 = mybir.dt.int32
+U32 = mybir.dt.uint32
+U16 = mybir.dt.uint16
+U8 = mybir.dt.uint8
+FP8X4 = mybir.dt.float8_e4m3fn_x4
+FP4X4 = mybir.dt.float4_e2m1fn_x4
+ALU = mybir.AluOpType
+HALF = S // 2
+
+
+def tile_picked_bilin_none_p_kernel(tc, x_words, x_scales, w1, fx, fy, offs, c00, c01, c10, c11, out):
+    nc = tc.nc
+    with ExitStack() as ctx:
+        pool = ctx.enter_context(tc.tile_pool(name="pool", bufs=1))
+        psum = ctx.enter_context(tc.psum_pool(name="psum", bufs=1))
+
+        picks = pool.tile([P, S // 16], U16, name="picks")
+        words = pool.tile([P, T], U16, name="words", align_bytes=64)
+        scales = pool.tile([P, T], U8, name="scales", align_bytes=64)
+        w_raw = pool.tile([P, 4, N], F32, name="w_raw")
+        fx_sb = pool.tile([P, V], F32, name="fx_sb")
+        fy_sb = pool.tile([P, V], F32, name="fy_sb")
+
+        nc.vector.memset(scales[:].bitcast(I32), 0)
+        nc.sync.dma_start(picks[:], offs)
+        nc.sync.dma_start(words[:].bitcast(I32), x_words[0].bitcast(I32))
+        nc.sync.dma_start(w_raw[:], w1.rearrange("(p j) m -> p j m", j=4))
+        for q in range(4):
+            nc.sync.dma_start(scales[32 * q : 32 * q + 4, :].bitcast(I32), x_scales[0, 4 * q : 4 * q + 4, :].bitcast(I32))
+        nc.sync.dma_start(fx_sb[:], fx)
+        nc.sync.dma_start(fy_sb[:], fy)
+        corners = []
+        for i, c in enumerate((c00, c01, c10, c11)):
+            t = pool.tile([P, V // 16], U16, name="corner%d" % i)
+            nc.sync.dma_start(t[:], c)
+            corners.append(t)
+
+        w_bf = pool.tile([P, N, 4], BF16, name="w_bf", align_bytes=64)
+        nc.scalar.copy(w_bf[:], w_raw[:].rearrange("p j m -> p m j"))
+
+        g_words = pool.tile([P, S], U16, name="g_words", align_bytes=64)
+        g_scales = pool.tile([P, S], U8, name="g_scales", align_bytes=64)
+        w_codes = pool.tile([P, N], U32, name="w_codes", align_bytes=64)
+        w_scales = pool.tile([P, N], U8, name="w_scales", align_bytes=64)
+        y = pool.tile([P, S], F32, name="y")
+
+        nc.vector.tensor_copy(g_words[:], words[:].indirect(picks[:]))
+        for h in range(2):
+            cols = slice(h * HALF, (h + 1) * HALF)
+            nc.vector.tensor_copy(g_scales[:, cols], scales[:].indirect(picks[:, h * HALF // 16 : (h + 1) * HALF // 16]))
+            if h == 0:
+                nc.vector.quantize_mx(out=w_codes[:].bitcast(FP8X4), scales=w_scales[:], in_=w_bf[:].rearrange("p m j -> p (m j)"))
+            acc = psum.tile([P, HALF], F32, name="acc%d" % h)
+            nc.tensor.matmul_mx(out=acc[:], lhsT=w_codes[:].bitcast(FP8X4), lhsT_scale=w_scales[:],
+                                rhs=g_words[:, cols].bitcast(FP4X4), rhs_scale=g_scales[:, cols], start=True, stop=True)
+            nc.scalar.copy(y[:, cols], acc[:])
+
+        wt = [pool.tile([P, V], F32, name="wt%d" % i) for i in range(4)]
+        nc.vector.scalar_tensor_tensor(wt[1][:], fy_sb[:], 1.0, fx_sb[:], ALU.subtract, ALU.mult)
+        nc.vector.scalar_tensor_tensor(wt[2][:], fx_sb[:], 1.0, fy_sb[:], ALU.subtract, ALU.mult)
+        nc.vector.tensor_tensor(wt[3][:], fx_sb[:], fy_sb[:], ALU.mult)
+        nc.vector.scalar_tensor_tensor(wt[0][:], wt[1][:], 1.0, fy_sb[:], ALU.add, ALU.subtract)
+
+        tm = [pool.tile([P, V], F32, name="tm%d" % i) for i in range(4)]
+        s0 = pool.tile([P, V], F32, name="s0")
+        s1 = pool.tile([P, V], F32, name="s1")
+        res = pool.tile([P, V], F32, name="res")
+
+        def term(i):
+            nc.vector.tensor_tensor(tm[i][:], y[:].indirect(corners[i][:]), wt[i][:], ALU.mult)
+
+        term(1)
+        term(0)
+        term(2)
+        nc.vector.tensor_tensor(s0[:], tm[0][:], tm[1][:], ALU.subtract)
+        term(3)
+        nc.vector.tensor_tensor(s1[:], s0[:], tm[2][:], ALU.subtract)
+        nc.vector.tensor_tensor(res[:], s1[:], tm[3][:], ALU.add)
+        nc.sync.dma_start(out, res[:])

@@ -15,7 +15,7 @@ U8 = mybir.dt.uint8
 FP8X4 = mybir.dt.float8_e4m3fn_x4
 FP4X4 = mybir.dt.float4_e2m1fn_x4
 ALU = mybir.AluOpType
-HALF = S // 2
+CUT = 192
 
 
 def tile_picked_bilin_none_p_kernel(tc, x_words, x_scales, w1, fx, fy, offs, c00, c01, c10, c11, out):
@@ -32,8 +32,8 @@ def tile_picked_bilin_none_p_kernel(tc, x_words, x_scales, w1, fx, fy, offs, c00
         fy_sb = pool.tile([P, V], F32, name="fy_sb")
 
         nc.vector.memset(scales[:].bitcast(I32), 0)
-        nc.sync.dma_start(picks[:], offs)
         nc.sync.dma_start(words[:].bitcast(I32), x_words[0].bitcast(I32))
+        nc.sync.dma_start(picks[:], offs)
         nc.sync.dma_start(w_raw[:], w1.rearrange("(p j) m -> p j m", j=4))
         for q in range(4):
             nc.sync.dma_start(scales[32 * q : 32 * q + 4, :].bitcast(I32), x_scales[0, 4 * q : 4 * q + 4, :].bitcast(I32))
@@ -46,7 +46,7 @@ def tile_picked_bilin_none_p_kernel(tc, x_words, x_scales, w1, fx, fy, offs, c00
             corners.append(t)
 
         w_bf = pool.tile([P, N, 4], BF16, name="w_bf", align_bytes=64)
-        nc.scalar.copy(w_bf[:], w_raw[:].rearrange("p j m -> p m j"))
+        nc.scalar.copy(w_bf[:].rearrange("p (c i) j -> p c j i", i=4), w_raw[:].rearrange("p j (c i) -> p c j i", i=4))
 
         g_words = pool.tile([P, S], U16, name="g_words", align_bytes=64)
         g_scales = pool.tile([P, S], U8, name="g_scales", align_bytes=64)
@@ -55,12 +55,12 @@ def tile_picked_bilin_none_p_kernel(tc, x_words, x_scales, w1, fx, fy, offs, c00
         y = pool.tile([P, S], F32, name="y")
 
         nc.vector.tensor_copy(g_words[:], words[:].indirect(picks[:]))
-        for h in range(2):
-            cols = slice(h * HALF, (h + 1) * HALF)
-            nc.vector.tensor_copy(g_scales[:, cols], scales[:].indirect(picks[:, h * HALF // 16 : (h + 1) * HALF // 16]))
+        for h, (lo, hi) in enumerate(((0, 256), (256, 384), (384, 512))):
+            cols = slice(lo, hi)
+            nc.vector.tensor_copy(g_scales[:, cols], scales[:].indirect(picks[:, lo // 16 : hi // 16]))
             if h == 0:
                 nc.vector.quantize_mx(out=w_codes[:].bitcast(FP8X4), scales=w_scales[:], in_=w_bf[:].rearrange("p m j -> p (m j)"))
-            acc = psum.tile([P, HALF], F32, name="acc%d" % h)
+            acc = psum.tile([P, hi - lo], F32, name="acc%d" % h)
             nc.tensor.matmul_mx(out=acc[:], lhsT=w_codes[:].bitcast(FP8X4), lhsT_scale=w_scales[:],
                                 rhs=g_words[:, cols].bitcast(FP4X4), rhs_scale=g_scales[:, cols], start=True, stop=True)
             nc.scalar.copy(y[:, cols], acc[:])
@@ -76,14 +76,16 @@ def tile_picked_bilin_none_p_kernel(tc, x_words, x_scales, w1, fx, fy, offs, c00
         s1 = pool.tile([P, V], F32, name="s1")
         res = pool.tile([P, V], F32, name="res")
 
-        def term(i):
-            nc.vector.tensor_tensor(tm[i][:], y[:].indirect(corners[i][:]), wt[i][:], ALU.mult)
+        def term(i, lo=0, hi=V):
+            nc.vector.tensor_tensor(tm[i][:, lo:hi], y[:].indirect(corners[i][:, lo // 16 : hi // 16]), wt[i][:, lo:hi], ALU.mult)
 
         term(1)
         term(0)
         term(2)
         nc.vector.tensor_tensor(s0[:], tm[0][:], tm[1][:], ALU.subtract)
-        term(3)
+        term(3, 0, CUT)
         nc.vector.tensor_tensor(s1[:], s0[:], tm[2][:], ALU.subtract)
-        nc.vector.tensor_tensor(res[:], s1[:], tm[3][:], ALU.add)
+        term(3, CUT, V)
+        for lo, hi in ((0, CUT), (CUT, V)):
+            nc.vector.tensor_tensor(res[:, lo:hi], s1[:, lo:hi], tm[3][:, lo:hi], ALU.add)
         nc.sync.dma_start(out, res[:])

@@ -31,19 +31,21 @@ def tile_picked_bilin_none_p_kernel(tc, x_words, x_scales, w1, fx, fy, offs, c00
         fx_sb = pool.tile([P, V], F32, name="fx_sb")
         fy_sb = pool.tile([P, V], F32, name="fy_sb")
 
+        corners = [pool.tile([P, V // 16], U16, name="corner%d" % i) for i in range(4)]
+
         nc.vector.memset(scales[:].bitcast(I32), 0)
         nc.sync.dma_start(words[:].bitcast(I32), x_words[0].bitcast(I32))
         nc.sync.dma_start(picks[:], offs)
         nc.sync.dma_start(w_raw[:], w1.rearrange("(p j) m -> p j m", j=4))
         for q in range(4):
             nc.sync.dma_start(scales[32 * q : 32 * q + 4, :].bitcast(I32), x_scales[0, 4 * q : 4 * q + 4, :].bitcast(I32))
-        nc.sync.dma_start(fx_sb[:], fx)
-        nc.sync.dma_start(fy_sb[:], fy)
-        corners = []
-        for i, c in enumerate((c00, c01, c10, c11)):
-            t = pool.tile([P, V // 16], U16, name="corner%d" % i)
-            nc.sync.dma_start(t[:], c)
-            corners.append(t)
+        nc.sync.dma_start(corners[1][:], c01)
+        for src, dst in ((fx, fx_sb), (fy, fy_sb)):
+            for lo in (0, V // 2):
+                nc.sync.dma_start(dst[:, lo : lo + V // 2], src[:, lo : lo + V // 2])
+        nc.sync.dma_start(corners[0][:], c00)
+        nc.sync.dma_start(corners[2][:], c10)
+        nc.sync.dma_start(corners[3][:], c11)
 
         w_bf = pool.tile([P, N, 4], BF16, name="w_bf", align_bytes=64)
         nc.scalar.copy(w_bf[:].rearrange("p (c i) j -> p c j i", i=4), w_raw[:].rearrange("p j (c i) -> p c j i", i=4))
@@ -71,21 +73,23 @@ def tile_picked_bilin_none_p_kernel(tc, x_words, x_scales, w1, fx, fy, offs, c00
         nc.vector.tensor_tensor(wt[3][:], fx_sb[:], fy_sb[:], ALU.mult)
         nc.vector.scalar_tensor_tensor(wt[0][:], wt[1][:], 1.0, fy_sb[:], ALU.add, ALU.subtract)
 
-        tm = [pool.tile([P, V], F32, name="tm%d" % i) for i in range(4)]
+        tm = [pool.tile([P, V], F32, name="tm%d" % i) for i in range(3)]
         s0 = pool.tile([P, V], F32, name="s0")
         s1 = pool.tile([P, V], F32, name="s1")
         res = pool.tile([P, V], F32, name="res")
 
-        def term(i, lo=0, hi=V):
-            nc.vector.tensor_tensor(tm[i][:, lo:hi], y[:].indirect(corners[i][:, lo // 16 : hi // 16]), wt[i][:, lo:hi], ALU.mult)
+        def term(i, dst, lo=0, hi=V):
+            nc.vector.tensor_tensor(dst, y[:].indirect(corners[i][:, lo // 16 : hi // 16]), wt[i][:, lo:hi], ALU.mult)
 
-        term(1)
-        term(0)
-        term(2)
+        term(1, tm[1][:])
+        term(0, tm[0][:])
+        term(2, tm[2][:])
         nc.vector.tensor_tensor(s0[:], tm[0][:], tm[1][:], ALU.subtract)
-        term(3, 0, CUT)
+        t3a = pool.tile([P, CUT], F32, name="wt0")
+        term(3, t3a[:], 0, CUT)
         nc.vector.tensor_tensor(s1[:], s0[:], tm[2][:], ALU.subtract)
-        term(3, CUT, V)
-        for lo, hi in ((0, CUT), (CUT, V)):
-            nc.vector.tensor_tensor(res[:, lo:hi], s1[:, lo:hi], tm[3][:, lo:hi], ALU.add)
+        t3b = pool.tile([P, V - CUT], F32, name="tm1")
+        term(3, t3b[:], CUT, V)
+        nc.vector.tensor_tensor(res[:, :CUT], s1[:, :CUT], t3a[:], ALU.add)
+        nc.vector.tensor_tensor(res[:, CUT:], s1[:, CUT:], t3b[:], ALU.add)
         nc.sync.dma_start(out, res[:])

@@ -15,7 +15,7 @@ U8 = mybir.dt.uint8
 FP8X4 = mybir.dt.float8_e4m3fn_x4
 FP4X4 = mybir.dt.float4_e2m1fn_x4
 ALU = mybir.AluOpType
-CUT = 192
+COPY = mybir.ActivationFunctionType.Copy
 
 
 def tile_picked_bilin_none_p_kernel(tc, x_words, x_scales, w1, fx, fy, offs, c00, c01, c10, c11, out):
@@ -43,8 +43,8 @@ def tile_picked_bilin_none_p_kernel(tc, x_words, x_scales, w1, fx, fy, offs, c00
         for src, dst in ((fx, fx_sb), (fy, fy_sb)):
             for lo in (0, V // 2):
                 nc.sync.dma_start(dst[:, lo : lo + V // 2], src[:, lo : lo + V // 2])
-        nc.sync.dma_start(corners[0][:], c00)
         nc.sync.dma_start(corners[2][:], c10)
+        nc.sync.dma_start(corners[0][:], c00)
         nc.sync.dma_start(corners[3][:], c11)
 
         w_bf = pool.tile([P, N, 4], BF16, name="w_bf", align_bytes=64)
@@ -73,23 +73,29 @@ def tile_picked_bilin_none_p_kernel(tc, x_words, x_scales, w1, fx, fy, offs, c00
         nc.vector.tensor_tensor(wt[3][:], fx_sb[:], fy_sb[:], ALU.mult)
         nc.vector.scalar_tensor_tensor(wt[0][:], wt[1][:], 1.0, fy_sb[:], ALU.add, ALU.subtract)
 
-        tm = [pool.tile([P, V], F32, name="tm%d" % i) for i in range(3)]
-        s0 = pool.tile([P, V], F32, name="s0")
+        def window(i):
+            return y[:].indirect(corners[i][:])
+
+        g0 = pool.tile([P, V], F32, name="g0")
+        g3 = pool.tile([P, V], F32, name="g3")
+        t1 = pool.tile([P, V], F32, name="t1")
+        t2 = pool.tile([P, V], F32, name="t2")
+        p0 = pool.tile([P, V], F32, name="p0")
+        p3 = pool.tile([P, V], F32, name="p3")
         s1 = pool.tile([P, V], F32, name="s1")
         res = pool.tile([P, V], F32, name="res")
 
-        def term(i, dst, lo=0, hi=V):
-            nc.vector.tensor_tensor(dst, y[:].indirect(corners[i][:, lo // 16 : hi // 16]), wt[i][:, lo:hi], ALU.mult)
-
-        term(1, tm[1][:])
-        term(0, tm[0][:])
-        term(2, tm[2][:])
-        nc.vector.tensor_tensor(s0[:], tm[0][:], tm[1][:], ALU.subtract)
-        t3a = pool.tile([P, CUT], F32, name="wt0")
-        term(3, t3a[:], 0, CUT)
-        nc.vector.tensor_tensor(s1[:], s0[:], tm[2][:], ALU.subtract)
-        t3b = pool.tile([P, V - CUT], F32, name="tm1")
-        term(3, t3b[:], CUT, V)
-        nc.vector.tensor_tensor(res[:, :CUT], s1[:, :CUT], t3a[:], ALU.add)
-        nc.vector.tensor_tensor(res[:, CUT:], s1[:, CUT:], t3b[:], ALU.add)
+        nc.scalar.activation(g0[:], window(0), COPY)
+        nc.scalar.activation(g3[:], window(3), COPY)
+        nc.vector.tensor_tensor(t1[:], window(1), wt[1][:], ALU.mult)
+        nc.vector.tensor_tensor(t2[:], window(2), wt[2][:], ALU.mult)
+        nc.vector.tensor_tensor(p0[:], g0[:], wt[0][:], ALU.mult)
+        nc.vector.tensor_tensor(p3[:], g3[:], wt[3][:], ALU.mult)
+        s0 = pool.tile([P, V], F32, name="y")
+        nc.vector.tensor_tensor(s0[:], p0[:], t1[:], ALU.subtract)
+        halves = (slice(0, V // 2), slice(V // 2, V))
+        for cols in halves:
+            nc.vector.tensor_tensor(s1[:, cols], p3[:, cols], t2[:, cols], ALU.subtract)
+        for cols in halves:
+            nc.vector.tensor_tensor(res[:, cols], s0[:, cols], s1[:, cols], ALU.add)
         nc.sync.dma_start(out, res[:])

@@ -16,6 +16,7 @@ FP8X4 = mybir.dt.float8_e4m3fn_x4
 FP4X4 = mybir.dt.float4_e2m1fn_x4
 ALU = mybir.AluOpType
 COPY = mybir.ActivationFunctionType.Copy
+CUT = 192
 
 
 def tile_picked_bilin_none_p_kernel(tc, x_words, x_scales, w1, fx, fy, offs, c00, c01, c10, c11, out):
@@ -73,29 +74,32 @@ def tile_picked_bilin_none_p_kernel(tc, x_words, x_scales, w1, fx, fy, offs, c00
         nc.vector.tensor_tensor(wt[3][:], fx_sb[:], fy_sb[:], ALU.mult)
         nc.vector.scalar_tensor_tensor(wt[0][:], wt[1][:], 1.0, fy_sb[:], ALU.add, ALU.subtract)
 
-        def window(i):
-            return y[:].indirect(corners[i][:])
+        def window(i, lo=0, hi=V):
+            return y[:].indirect(corners[i][:, lo // 16 : hi // 16])
 
         g0 = pool.tile([P, V], F32, name="g0")
+        g2 = pool.tile([P, V - CUT], F32, name="g2")
         g3 = pool.tile([P, V], F32, name="g3")
         t1 = pool.tile([P, V], F32, name="t1")
         t2 = pool.tile([P, V], F32, name="t2")
         p0 = pool.tile([P, V], F32, name="p0")
         p3 = pool.tile([P, V], F32, name="p3")
+        s0 = pool.tile([P, V], F32, name="s0")
         s1 = pool.tile([P, V], F32, name="s1")
         res = pool.tile([P, V], F32, name="res")
 
+        nc.scalar.activation(g2[:], window(2, CUT, V), COPY)
         nc.scalar.activation(g0[:], window(0), COPY)
         nc.scalar.activation(g3[:], window(3), COPY)
         nc.vector.tensor_tensor(t1[:], window(1), wt[1][:], ALU.mult)
-        nc.vector.tensor_tensor(t2[:], window(2), wt[2][:], ALU.mult)
+        nc.vector.tensor_tensor(t2[:, :CUT], window(2, 0, CUT), wt[2][:, :CUT], ALU.mult)
+        nc.vector.tensor_tensor(t2[:, CUT:], g2[:], wt[2][:, CUT:], ALU.mult)
         nc.vector.tensor_tensor(p0[:], g0[:], wt[0][:], ALU.mult)
+        nc.vector.tensor_tensor(s0[:], t1[:], t2[:], ALU.add)
         nc.vector.tensor_tensor(p3[:], g3[:], wt[3][:], ALU.mult)
-        s0 = pool.tile([P, V], F32, name="y")
-        nc.vector.tensor_tensor(s0[:], p0[:], t1[:], ALU.subtract)
-        halves = (slice(0, V // 2), slice(V // 2, V))
-        for cols in halves:
-            nc.vector.tensor_tensor(s1[:, cols], p3[:, cols], t2[:, cols], ALU.subtract)
-        for cols in halves:
-            nc.vector.tensor_tensor(res[:, cols], s0[:, cols], s1[:, cols], ALU.add)
+        parts = [slice(lo, lo + V // 4) for lo in range(0, V, V // 4)]
+        for cols in parts:
+            nc.vector.tensor_tensor(s1[:, cols], p0[:, cols], s0[:, cols], ALU.subtract)
+        for cols in parts:
+            nc.vector.tensor_tensor(res[:, cols], s1[:, cols], p3[:, cols], ALU.add)
         nc.sync.dma_start(out, res[:])

@@ -16,7 +16,6 @@ FP8X4 = mybir.dt.float8_e4m3fn_x4
 FP4X4 = mybir.dt.float4_e2m1fn_x4
 ALU = mybir.AluOpType
 COPY = mybir.ActivationFunctionType.Copy
-CUT = 192
 
 
 def tile_picked_bilin_none_p_kernel(tc, x_words, x_scales, w1, fx, fy, offs, c00, c01, c10, c11, out):
@@ -74,11 +73,11 @@ def tile_picked_bilin_none_p_kernel(tc, x_words, x_scales, w1, fx, fy, offs, c00
         nc.vector.tensor_tensor(wt[3][:], fx_sb[:], fy_sb[:], ALU.mult)
         nc.vector.scalar_tensor_tensor(wt[0][:], wt[1][:], 1.0, fy_sb[:], ALU.add, ALU.subtract)
 
-        def window(i, lo=0, hi=V):
-            return y[:].indirect(corners[i][:, lo // 16 : hi // 16])
+        def window(i, cols):
+            return y[:].indirect(corners[i][:, cols.start // 16 : cols.stop // 16])
 
         g0 = pool.tile([P, V], F32, name="g0")
-        g2 = pool.tile([P, V - CUT], F32, name="g2")
+        g2 = pool.tile([P, V], F32, name="g2")
         g3 = pool.tile([P, V], F32, name="g3")
         t1 = pool.tile([P, V], F32, name="t1")
         t2 = pool.tile([P, V], F32, name="t2")
@@ -87,19 +86,32 @@ def tile_picked_bilin_none_p_kernel(tc, x_words, x_scales, w1, fx, fy, offs, c00
         s0 = pool.tile([P, V], F32, name="s0")
         s1 = pool.tile([P, V], F32, name="s1")
         res = pool.tile([P, V], F32, name="res")
+        a, b = slice(0, V // 2), slice(V // 2, V)
+        b1, b2 = slice(V // 2, 3 * V // 4), slice(3 * V // 4, V)
 
-        nc.scalar.activation(g2[:], window(2, CUT, V), COPY)
-        nc.scalar.activation(g0[:], window(0), COPY)
-        nc.scalar.activation(g3[:], window(3), COPY)
-        nc.vector.tensor_tensor(t1[:], window(1), wt[1][:], ALU.mult)
-        nc.vector.tensor_tensor(t2[:, :CUT], window(2, 0, CUT), wt[2][:, :CUT], ALU.mult)
-        nc.vector.tensor_tensor(t2[:, CUT:], g2[:], wt[2][:, CUT:], ALU.mult)
-        nc.vector.tensor_tensor(p0[:], g0[:], wt[0][:], ALU.mult)
-        nc.vector.tensor_tensor(s0[:], t1[:], t2[:], ALU.add)
-        nc.vector.tensor_tensor(p3[:], g3[:], wt[3][:], ALU.mult)
-        parts = [slice(lo, lo + V // 4) for lo in range(0, V, V // 4)]
-        for cols in parts:
-            nc.vector.tensor_tensor(s1[:, cols], p0[:, cols], s0[:, cols], ALU.subtract)
-        for cols in parts:
-            nc.vector.tensor_tensor(res[:, cols], s1[:, cols], p3[:, cols], ALU.add)
+        def fetch(dst, i, cols):
+            nc.scalar.activation(dst[:, cols], window(i, cols), COPY)
+
+        def combine(dst, left, right, op, cols):
+            nc.vector.tensor_tensor(dst[:, cols], left[:, cols], right[:, cols], op)
+
+        fetch(g2, 2, b)
+        fetch(g0, 0, a)
+        fetch(g0, 0, b)
+        fetch(g3, 3, a)
+        fetch(g3, 3, b)
+        nc.vector.tensor_tensor(t1[:], window(1, slice(0, V)), wt[1][:], ALU.mult)
+        nc.vector.tensor_tensor(t2[:, a], window(2, a), wt[2][:, a], ALU.mult)
+        combine(t2, g2, wt[2], ALU.mult, b)
+        combine(p0, g0, wt[0], ALU.mult, a)
+        combine(s0, t1, t2, ALU.add, a)
+        combine(p0, g0, wt[0], ALU.mult, b)
+        combine(s0, t1, t2, ALU.add, b)
+        combine(s1, p0, s0, ALU.subtract, a)
+        combine(p3, g3, wt[3], ALU.mult, a)
+        combine(s1, p0, s0, ALU.subtract, b)
+        combine(p3, g3, wt[3], ALU.mult, b1)
+        combine(p3, g3, wt[3], ALU.mult, b2)
+        for cols in (a, b1, b2):
+            combine(res, s1, p3, ALU.add, cols)
         nc.sync.dma_start(out, res[:])

@@ -40,9 +40,9 @@ def tile_picked_bilin_none_p_kernel(tc, x_words, x_scales, w1, fx, fy, offs, c00
         for q in range(4):
             nc.sync.dma_start(scales[32 * q : 32 * q + 4, :].bitcast(I32), x_scales[0, 4 * q : 4 * q + 4, :].bitcast(I32))
         nc.sync.dma_start(corners[1][:], c01)
-        for src, dst in ((fx, fx_sb), (fy, fy_sb)):
-            for lo in (0, V // 2):
-                nc.sync.dma_start(dst[:, lo : lo + V // 2], src[:, lo : lo + V // 2])
+        for lo in (0, V // 2):
+            nc.sync.dma_start(fx_sb[:, lo : lo + V // 2], fx[:, lo : lo + V // 2])
+        nc.sync.dma_start(fy_sb[:], fy)
         nc.sync.dma_start(corners[2][:], c10)
         nc.sync.dma_start(corners[0][:], c00)
         nc.sync.dma_start(corners[3][:], c11)
@@ -114,4 +114,5 @@ def tile_picked_bilin_none_p_kernel(tc, x_words, x_scales, w1, fx, fy, offs, c00
         combine(p3, g3, wt[3], ALU.mult, b2)
         for cols in (a, b1, b2):
             combine(res, s1, p3, ALU.add, cols)
-        nc.sync.dma_start(out, res[:])
+        for cols in (a, b):
+            nc.sync.dma_start(out[:, cols], res[:, cols])

@@ -87,7 +87,6 @@ def tile_picked_bilin_none_p_kernel(tc, x_words, x_scales, w1, fx, fy, offs, c00
         s1 = pool.tile([P, V], F32, name="s1")
         res = pool.tile([P, V], F32, name="res")
         a, b = slice(0, V // 2), slice(V // 2, V)
-        b1, b2 = slice(V // 2, 3 * V // 4), slice(3 * V // 4, V)
 
         def fetch(dst, i, cols):
             nc.scalar.activation(dst[:, cols], window(i, cols), COPY)
@@ -110,9 +109,9 @@ def tile_picked_bilin_none_p_kernel(tc, x_words, x_scales, w1, fx, fy, offs, c00
         combine(s1, p0, s0, ALU.subtract, a)
         combine(p3, g3, wt[3], ALU.mult, a)
         combine(s1, p0, s0, ALU.subtract, b)
-        combine(p3, g3, wt[3], ALU.mult, b1)
-        combine(p3, g3, wt[3], ALU.mult, b2)
-        for cols in (a, b1, b2):
+        combine(p3, g3, wt[3], ALU.mult, slice(128, 176))
+        combine(p3, g3, wt[3], ALU.mult, slice(176, 256))
+        for cols in (slice(0, 96), slice(96, 176), slice(176, 256)):
             combine(res, s1, p3, ALU.add, cols)
-        for cols in (a, b):
+        for cols in (slice(0, 96), slice(96, 256)):
             nc.sync.dma_start(out[:, cols], res[:, cols])

@@ -36,12 +36,12 @@ def tile_picked_bilin_none_p_kernel(tc, x_words, x_scales, w1, fx, fy, offs, c00
         nc.vector.memset(scales[:].bitcast(I32), 0)
         nc.sync.dma_start(words[:].bitcast(I32), x_words[0].bitcast(I32))
         nc.sync.dma_start(picks[:], offs)
+        nc.sync.dma_start(corners[1][:], c01)
         nc.sync.dma_start(w_raw[:], w1.rearrange("(p j) m -> p j m", j=4))
         for q in range(4):
             nc.sync.dma_start(scales[32 * q : 32 * q + 4, :].bitcast(I32), x_scales[0, 4 * q : 4 * q + 4, :].bitcast(I32))
-        nc.sync.dma_start(corners[1][:], c01)
-        for lo in (0, V // 2):
-            nc.sync.dma_start(fx_sb[:, lo : lo + V // 2], fx[:, lo : lo + V // 2])
+        nc.sync.dma_start(fx_sb[:, 0:128], fx[:, 0:128])
+        nc.sync.dma_start(fx_sb[:, 128:256], fx[:, 128:256])
         nc.sync.dma_start(fy_sb[:], fy)
         nc.sync.dma_start(corners[2][:], c10)
         nc.sync.dma_start(corners[0][:], c00)
@@ -69,9 +69,9 @@ def tile_picked_bilin_none_p_kernel(tc, x_words, x_scales, w1, fx, fy, offs, c00
 
         wt = [pool.tile([P, V], F32, name="wt%d" % i) for i in range(4)]
         nc.vector.scalar_tensor_tensor(wt[1][:], fy_sb[:], 1.0, fx_sb[:], ALU.subtract, ALU.mult)
-        nc.vector.scalar_tensor_tensor(wt[2][:], fx_sb[:], 1.0, fy_sb[:], ALU.subtract, ALU.mult)
         nc.vector.tensor_tensor(wt[3][:], fx_sb[:], fy_sb[:], ALU.mult)
         nc.vector.scalar_tensor_tensor(wt[0][:], wt[1][:], 1.0, fy_sb[:], ALU.add, ALU.subtract)
+        nc.vector.scalar_tensor_tensor(wt[2][:], fx_sb[:], 1.0, fy_sb[:], ALU.subtract, ALU.mult)
 
         def window(i, cols):
             return y[:].indirect(corners[i][:, cols.start // 16 : cols.stop // 16])

@@ -25,11 +25,11 @@ def tile_picked_bilin_none_p_kernel(tc, x_words, x_scales, w1, fx, fy, offs, c00
         psum = ctx.enter_context(tc.psum_pool(name="psum", bufs=1))
 
         picks = pool.tile([P, S // 16], U16, name="picks")
-        words = pool.tile([P, T], U16, name="words", align_bytes=64)
-        scales = pool.tile([P, T], U8, name="scales", align_bytes=64)
-        w_raw = pool.tile([P, 4, N], F32, name="w_raw")
-        fx_sb = pool.tile([P, V], F32, name="fx_sb")
-        fy_sb = pool.tile([P, V], F32, name="fy_sb")
+        words = pool.tile([P, T], U16, name="words", align_bytes=256)
+        scales = pool.tile([P, T], U8, name="scales", align_bytes=256)
+        w_raw = pool.tile([P, 4, N], F32, name="w_raw", align_bytes=256)
+        fx_sb = pool.tile([P, V], F32, name="fx_sb", align_bytes=256)
+        fy_sb = pool.tile([P, V], F32, name="fy_sb", align_bytes=256)
 
         corners = [pool.tile([P, V // 16], U16, name="corner%d" % i) for i in range(4)]
 
@@ -47,14 +47,14 @@ def tile_picked_bilin_none_p_kernel(tc, x_words, x_scales, w1, fx, fy, offs, c00
         nc.sync.dma_start(corners[0][:], c00)
         nc.sync.dma_start(corners[3][:], c11)
 
-        w_bf = pool.tile([P, N, 4], BF16, name="w_bf", align_bytes=64)
+        w_bf = pool.tile([P, N, 4], BF16, name="w_bf", align_bytes=256)
         nc.scalar.copy(w_bf[:].rearrange("p (c i) j -> p c j i", i=4), w_raw[:].rearrange("p j (c i) -> p c j i", i=4))
 
-        g_words = pool.tile([P, S], U16, name="g_words", align_bytes=64)
-        g_scales = pool.tile([P, S], U8, name="g_scales", align_bytes=64)
-        w_codes = pool.tile([P, N], U32, name="w_codes", align_bytes=64)
-        w_scales = pool.tile([P, N], U8, name="w_scales", align_bytes=64)
-        y = pool.tile([P, S], F32, name="y")
+        g_words = pool.tile([P, S], U16, name="g_words", align_bytes=256)
+        g_scales = pool.tile([P, S], U8, name="g_scales", align_bytes=256)
+        w_codes = pool.tile([P, N], U32, name="w_codes", align_bytes=256)
+        w_scales = pool.tile([P, N], U8, name="w_scales", align_bytes=256)
+        y = pool.tile([P, S], F32, name="y", align_bytes=256)
 
         nc.vector.tensor_copy(g_words[:], words[:].indirect(picks[:]))
         for h, (lo, hi) in enumerate(((0, 256), (256, 384), (384, 512))):
@@ -85,7 +85,7 @@ def tile_picked_bilin_none_p_kernel(tc, x_words, x_scales, w1, fx, fy, offs, c00
         p3 = pool.tile([P, V], F32, name="p3")
         s0 = pool.tile([P, V], F32, name="s0")
         s1 = pool.tile([P, V], F32, name="s1")
-        res = pool.tile([P, V], F32, name="res")
+        res = pool.tile([P, V], F32, name="res", align_bytes=256)
         a, b = slice(0, V // 2), slice(V // 2, V)
 
         def fetch(dst, i, cols):

@@ -24,14 +24,14 @@ def tile_picked_bilin_none_p_kernel(tc, x_words, x_scales, w1, fx, fy, offs, c00
         pool = ctx.enter_context(tc.tile_pool(name="pool", bufs=1))
         psum = ctx.enter_context(tc.psum_pool(name="psum", bufs=1))
 
-        picks = pool.tile([P, S // 16], U16, name="picks")
+        picks = pool.tile([P, S // 16], U16, name="picks", align_bytes=256)
         words = pool.tile([P, T], U16, name="words", align_bytes=256)
         scales = pool.tile([P, T], U8, name="scales", align_bytes=256)
         w_raw = pool.tile([P, 4, N], F32, name="w_raw", align_bytes=256)
         fx_sb = pool.tile([P, V], F32, name="fx_sb", align_bytes=256)
         fy_sb = pool.tile([P, V], F32, name="fy_sb", align_bytes=256)
 
-        corners = [pool.tile([P, V // 16], U16, name="corner%d" % i) for i in range(4)]
+        corners = [pool.tile([P, V // 16], U16, name="corner%d" % i, align_bytes=256) for i in range(4)]
 
         nc.vector.memset(scales[:].bitcast(I32), 0)
         nc.sync.dma_start(words[:].bitcast(I32), x_words[0].bitcast(I32))
@@ -109,9 +109,9 @@ def tile_picked_bilin_none_p_kernel(tc, x_words, x_scales, w1, fx, fy, offs, c00
         combine(s1, p0, s0, ALU.subtract, a)
         combine(p3, g3, wt[3], ALU.mult, a)
         combine(s1, p0, s0, ALU.subtract, b)
-        combine(p3, g3, wt[3], ALU.mult, slice(128, 176))
-        combine(p3, g3, wt[3], ALU.mult, slice(176, 256))
-        for cols in (slice(0, 96), slice(96, 176), slice(176, 256)):
+        combine(p3, g3, wt[3], ALU.mult, slice(128, 192))
+        combine(p3, g3, wt[3], ALU.mult, slice(192, 256))
+        for cols in (slice(0, 128), slice(128, 192), slice(192, 256)):
             combine(res, s1, p3, ALU.add, cols)
-        for cols in (slice(0, 96), slice(96, 256)):
+        for cols in (slice(0, 128), slice(128, 256)):
             nc.sync.dma_start(out[:, cols], res[:, cols])

from contextlib import ExitStack

import concourse.mybir as mybir

K, T, S, V, N = 512, 1024, 512, 256, 128
P = 128
FLOPS = 2 * K * N * S

F32 = mybir.dt.float32
BF16 = mybir.dt.bfloat16
I32 = mybir.dt.int32
U32 = mybir.dt.uint32
U16 = mybir.dt.uint16
U8 = mybir.dt.uint8
FP8X4 = mybir.dt.float8_e4m3fn_x4
FP4X4 = mybir.dt.float4_e2m1fn_x4
ALU = mybir.AluOpType
COPY = mybir.ActivationFunctionType.Copy


def tile_picked_bilin_none_p_kernel(tc, x_words, x_scales, w1, fx, fy, offs, c00, c01, c10, c11, out):
    nc = tc.nc
    with ExitStack() as ctx:
        pool = ctx.enter_context(tc.tile_pool(name="pool", bufs=1))
        psum = ctx.enter_context(tc.psum_pool(name="psum", bufs=1))

        picks = pool.tile([P, S // 16], U16, name="picks", align_bytes=256)
        words = pool.tile([P, T], U16, name="words", align_bytes=256)
        scales = pool.tile([P, T], U8, name="scales", align_bytes=256)
        w_raw = pool.tile([P, 4, N], F32, name="w_raw", align_bytes=256)
        fx_sb = pool.tile([P, V], F32, name="fx_sb", align_bytes=256)
        fy_sb = pool.tile([P, V], F32, name="fy_sb", align_bytes=256)

        corners = [pool.tile([P, V // 16], U16, name="corner%d" % i, align_bytes=256) for i in range(4)]

        nc.vector.memset(scales[:].bitcast(I32), 0)
        nc.sync.dma_start(words[:].bitcast(I32), x_words[0].bitcast(I32))
        nc.sync.dma_start(picks[:], offs)
        nc.sync.dma_start(corners[1][:], c01)
        nc.sync.dma_start(w_raw[:], w1.rearrange("(p j) m -> p j m", j=4))
        for q in range(4):
            nc.sync.dma_start(scales[32 * q : 32 * q + 4, :].bitcast(I32), x_scales[0, 4 * q : 4 * q + 4, :].bitcast(I32))
        nc.sync.dma_start(fx_sb[:, 0:128], fx[:, 0:128])
        nc.sync.dma_start(fx_sb[:, 128:256], fx[:, 128:256])
        nc.sync.dma_start(fy_sb[:], fy)
        nc.sync.dma_start(corners[2][:], c10)
        nc.sync.dma_start(corners[0][:], c00)
        nc.sync.dma_start(corners[3][:], c11)

        w_bf = pool.tile([P, N, 4], BF16, name="w_bf", align_bytes=256)
        nc.scalar.copy(w_bf[:].rearrange("p (c i) j -> p c j i", i=4), w_raw[:].rearrange("p j (c i) -> p c j i", i=4))

        g_words = pool.tile([P, S], U16, name="g_words", align_bytes=256)
        g_scales = pool.tile([P, S], U8, name="g_scales", align_bytes=256)
        w_codes = pool.tile([P, N], U32, name="w_codes", align_bytes=256)
        w_scales = pool.tile([P, N], U8, name="w_scales", align_bytes=256)
        y = pool.tile([P, S], F32, name="y", align_bytes=256)

        nc.vector.tensor_copy(g_words[:], words[:].indirect(picks[:]))
        for h, (lo, hi) in enumerate(((0, 256), (256, 384), (384, 512))):
            cols = slice(lo, hi)
            nc.vector.tensor_copy(g_scales[:, cols], scales[:].indirect(picks[:, lo // 16 : hi // 16]))
            if h == 0:
                nc.vector.quantize_mx(out=w_codes[:].bitcast(FP8X4), scales=w_scales[:], in_=w_bf[:].rearrange("p m j -> p (m j)"))
            acc = psum.tile([P, hi - lo], F32, name="acc%d" % h)
            nc.tensor.matmul_mx(out=acc[:], lhsT=w_codes[:].bitcast(FP8X4), lhsT_scale=w_scales[:],
                                rhs=g_words[:, cols].bitcast(FP4X4), rhs_scale=g_scales[:, cols], start=True, stop=True)
            nc.scalar.copy(y[:, cols], acc[:])

        wt = [pool.tile([P, V], F32, name="wt%d" % i) for i in range(4)]
        nc.vector.scalar_tensor_tensor(wt[1][:], fy_sb[:], 1.0, fx_sb[:], ALU.subtract, ALU.mult)
        nc.vector.tensor_tensor(wt[3][:], fx_sb[:], fy_sb[:], ALU.mult)
        nc.vector.scalar_tensor_tensor(wt[0][:], wt[1][:], 1.0, fy_sb[:], ALU.add, ALU.subtract)
        nc.vector.scalar_tensor_tensor(wt[2][:], fx_sb[:], 1.0, fy_sb[:], ALU.subtract, ALU.mult)

        def window(i, cols):
            return y[:].indirect(corners[i][:, cols.start // 16 : cols.stop // 16])

        g0 = pool.tile([P, V], F32, name="g0")
        g2 = pool.tile([P, V], F32, name="g2")
        g3 = pool.tile([P, V], F32, name="g3")
        t1 = pool.tile([P, V], F32, name="t1")
        t2 = pool.tile([P, V], F32, name="t2")
        p0 = pool.tile([P, V], F32, name="p0")
        p3 = pool.tile([P, V], F32, name="p3")
        s0 = pool.tile([P, V], F32, name="s0")
        s1 = pool.tile([P, V], F32, name="s1")
        res = pool.tile([P, V], F32, name="res", align_bytes=256)
        a, b = slice(0, V // 2), slice(V // 2, V)

        def fetch(dst, i, cols):
            nc.scalar.activation(dst[:, cols], window(i, cols), COPY)

        def combine(dst, left, right, op, cols):
            nc.vector.tensor_tensor(dst[:, cols], left[:, cols], right[:, cols], op)

        fetch(g2, 2, b)
        fetch(g0, 0, a)
        fetch(g0, 0, b)
        fetch(g3, 3, a)
        fetch(g3, 3, b)
        nc.vector.tensor_tensor(t1[:], window(1, slice(0, V)), wt[1][:], ALU.mult)
        nc.vector.tensor_tensor(t2[:, a], window(2, a), wt[2][:, a], ALU.mult)
        combine(t2, g2, wt[2], ALU.mult, b)
        combine(p0, g0, wt[0], ALU.mult, a)
        combine(s0, t1, t2, ALU.add, a)
        combine(p0, g0, wt[0], ALU.mult, b)
        combine(s0, t1, t2, ALU.add, b)
        combine(s1, p0, s0, ALU.subtract, a)
        combine(p3, g3, wt[3], ALU.mult, a)
        combine(s1, p0, s0, ALU.subtract, b)
        combine(p3, g3, wt[3], ALU.mult, slice(128, 192))
        combine(p3, g3, wt[3], ALU.mult, slice(192, 256))
        for cols in (slice(0, 128), slice(128, 192), slice(192, 256)):
            combine(res, s1, p3, ALU.add, cols)
        for cols in (slice(0, 128), slice(128, 256)):
            nc.sync.dma_start(out[:, cols], res[:, cols])
